import numpy as np
import ml_dtypes


def mxq(x, axis, fmt="e4m3"):
    dtype, down = {"e4m3": (ml_dtypes.float8_e4m3fn, 7), "e5m2": (ml_dtypes.float8_e5m2, 14)}[fmt]
    v = np.moveaxis(np.asarray(x, np.float32).astype(ml_dtypes.bfloat16).astype(np.float64), axis, -1)
    blocks = v.reshape(v.shape[:-1] + (-1, 32))
    amax = np.abs(blocks).max(-1, keepdims=True)
    byte = np.maximum(np.where(amax > 0, np.frexp(amax)[1] - 1 + 127, 0) - down, 1)
    scale = np.exp2(byte - 127.0)
    codes = (blocks / scale).astype(np.float32).astype(dtype).astype(np.float64)
    return np.moveaxis((codes * scale).reshape(v.shape), -1, axis)


WIDE = False


def mx_kscale(k):
    if not WIDE:
        return np.ones(k)
    levels = np.array([10, -10, 5, -5, 0])
    if k % 512:
        return np.exp2(np.random.permutation(np.resize(levels, k // 32))).repeat(32)
    a = np.empty((k // 512, 16))
    for p in range(k // 512):
        a[p, :8] = np.random.permutation(np.resize(levels, 8))
        for g in range(8):
            far = levels[np.abs(levels - a[p, g]) >= 10]
            a[p, g + 8] = far[np.random.randint(len(far))]
    return np.exp2(a.ravel()).repeat(32)


def f64(x):
    return np.asarray(x).astype(np.float64)


def striped(idx):
    return np.tile(idx.reshape(-1, 16).T, (8, 1)).astype(np.uint16)


def unstriped(offs):
    return offs[:16].T.reshape(-1).astype(np.int64)


def pack_weight(w):
    k, n = w.shape
    w = f64(np.asarray(w, np.float32).astype(ml_dtypes.bfloat16)).reshape(k // 32, 32, n)
    amax = np.abs(w).max(1)
    byte = np.clip(np.where(amax > 0, np.frexp(amax)[1] - 1 + 127 - 7, 1), 1, 254)
    scaled = (w * np.exp2(127.0 - byte)[:, None, :]).reshape(k, n).astype(np.float32)
    words = np.ascontiguousarray(scaled.reshape(k // 512, 128, 4, n).transpose(0, 1, 3, 2)).astype(ml_dtypes.float8_e4m3fn).view(np.uint8)
    return words, np.ascontiguousarray(byte.astype(np.uint8).reshape(k // 512, 16, n))


def unpack_weight(words, scales):
    g, p, n, _ = words.shape
    vals = np.ascontiguousarray(words).view(ml_dtypes.float8_e4m3fn).astype(np.float64) * np.repeat(np.exp2(scales.astype(np.float64) - 127.0), 8, axis=1)[..., None]
    return vals.transpose(0, 1, 3, 2).reshape(g * 512, n)


def silu(v):
    return v / (1.0 + np.exp(-np.maximum(v, -700.0)))


K, T, H, N = 1024, 512, 512, 128


def setup_inputs():
    n = np.random.standard_normal
    s = mx_kscale(K)[:, None]
    u = mx_kscale(H)
    packed_xT = pack_weight(n((K, T)) * s)
    return {
        "x_words": packed_xT[0],
        "x_scales": packed_xT[1],
        "w1": (n((K, H)) / np.sqrt(2 * K) / s * u).astype(np.float32),
        "w2": (n((K, H)) / np.sqrt(2 * K) / s * u).astype(np.float32),
        "w3": (n((H, N)) / np.sqrt(H) / u[:, None]).astype(np.float32),
        "pos1": striped(np.random.permutation(T)),
        "pos2": striped(np.random.permutation(T)),
        "pos3": striped(np.random.permutation(T)),
        "pos4": striped(np.random.permutation(T)),
    }


def reference(x_words, x_scales, w1, w2, w3, pos1, pos2, pos3, pos4):
    xq = unpack_weight(x_words, x_scales)
    y = mxq(f64(w1), 0, "e4m3").T @ xq
    e = mxq(f64(w2), 0, "e4m3").T @ xq
    z = np.maximum(np.maximum(np.maximum(silu(y + e[:, unstriped(pos1)]), silu(y + e[:, unstriped(pos2)])), silu(y + e[:, unstriped(pos3)])), silu(y + e[:, unstriped(pos4)]))
    return mxq(f64(w3), 0, "e4m3").T @ mxq(z, 0, "e4m3")

@@ -1,0 +1,325 @@
+from contextlib import ExitStack
+
+import concourse.mybir as mybir
+from concourse.masks import make_identity
+
+K, T, H, N = 1024, 512, 512, 128
+FLOPS = 2 * (2 * K * H * T + H * N * T)
+
+F32 = mybir.dt.float32
+BF16 = mybir.dt.bfloat16
+I32 = mybir.dt.int32
+U32 = mybir.dt.uint32
+U16 = mybir.dt.uint16
+U8 = mybir.dt.uint8
+FP8X4 = mybir.dt.float8_e4m3fn_x4
+SILU = mybir.ActivationFunctionType.Silu
+MAX = mybir.AluOpType.max
+
+P = 128
+PACK = 4
+PASSES = K // (P * PACK)
+TILES = H // P
+WINDOW = 704
+CHUNK = 256
+
+OPT = {
+ "head": 2,
+ "dmin": 0,
+ "sq": 1,
+ "e": 4,
+ "et": 0,
+ "tailw": 128,
+ "prod": 3,
+ "ytag": "y11",
+ "loads": "l0 y0 l1 e1 y1 l2 l3 e2 y2 e3 y3",
+ "tags": "- e11 - - - y20 y21 y30 y31 w3 p5 p6 p7 p8 p9 p10 p13 p14 p15 p16 p17 p18 p19 p20",
+ "pre": "v000 q001 v001 q011 m00 e00 v010 c011 q022 m01 c100 c101 q102 m10 c110 c111 q122 m11 e01 c200 e10 c201 e11 c212 q204 m20 m21 c302 c312 q304 w e20 e21 g00 g01 m30 e30 g02 m31 e31 g03 A0 B0 g10 g11 g12 g13 A1 B1 g20 g21 g22 g23"
+}
+
+
+def tile_picked_wedgecv_silu_l_kernel(
+    tc, x_words, x_scales, w1, w2, w3, pos1, pos2, pos3, pos4, out
+):
+    nc = tc.nc
+    with ExitStack() as ctx:
+        held = ctx.enter_context(tc.tile_pool(name="held", bufs=1))
+        products = ctx.enter_context(tc.psum_pool(name="products", bufs=OPT["prod"]))
+        edges = ctx.enter_context(tc.psum_pool(name="edges", bufs=1))
+
+        def tile(shape, dtype, name, tag=None):
+            return held.tile(shape, dtype, name=name, tag=tag or name, align_bytes=64)
+
+        x_planes = tile([P, PASSES, T], U8, "x_planes")
+        nc.gpsimd.memset(x_planes[:].rearrange("p z c -> p (z c)").bitcast(I32), 0)
+        for quad in range(4):
+            (nc.scalar if OPT["sq"] else nc.sync).dma_start(
+                out=x_planes[32 * quad : 32 * quad + 4, :, :].bitcast(I32),
+                in_=x_scales[:, 4 * quad : 4 * quad + 4, :].rearrange("z r c -> r z c").bitcast(I32),
+            )
+
+        raw = {}
+        slots = {}
+
+        def load_weight(name, w, first, count):
+            staged = tile([P, PASSES * PACK * P], F32, "raw_%s_%d" % (name, first))
+            for z in range(PASSES):
+                rows = w[z * P * PACK : (z + 1) * P * PACK, first * P : (first + 1) * P]
+                part = staged[:, z * T : (z + 1) * T]
+                nc.sync.dma_start(out=part.rearrange("p (j c) -> p j c", j=PACK), in_=rows.rearrange("(p j) c -> p j c", j=PACK))
+                slots["%s%d%d" % ({"w2": "e", "w1": "y"}[name], first, z)] = part
+            raw[name, first] = staged
+
+        lists = []
+
+        def load_list(pos):
+            offsets = held.tile([P, T // 16], U16, name="list_%d" % len(lists))
+            nc.sync.dma_start(offsets[:], pos)
+            lists.append(offsets)
+
+        load_weight("w2", w2, 0, 1)
+        x_codes = []
+        for z in range(PASSES):
+            words = tile([P, T], U32, "x_codes_%d" % z)
+            nc.sync.dma_start(
+                out=words[:].bitcast(I32), in_=x_words[z].rearrange("p n t -> p (n t)").bitcast(I32)
+            )
+            x_codes.append(words)
+        for step in OPT["loads"].split():
+            if step[0] == "l":
+                load_list([pos1, pos2, pos3, pos4][int(step[1])])
+            elif step[0] == "e":
+                load_weight("w2", w2, int(step[1]), 1)
+            else:
+                load_weight("w1", w1, int(step[1]), 1)
+        raw_w3 = tile([P, PACK, N], F32, "raw_w3")
+        nc.sync.dma_start(out=raw_w3[:], in_=w3.rearrange("(p j) c -> p j c", j=PACK))
+
+        e_tiles = []
+        for q in range(TILES):
+            e_sb = tile([P, WINDOW], F32, "e_%d" % q)
+            nc.gpsimd.memset(e_sb[:, T:], 0.0)
+            e_tiles.append(e_sb)
+
+        slots["w3"] = raw_w3[:].rearrange("p j c -> p (j c)")
+        identity = tile([P, P], F32, "identity")
+        make_identity(nc, identity[:])
+        warm = tile([P, 1], F32, "warm")
+        nc.scalar.activation(warm[:], e_tiles[0][:, T : T + 1], SILU)
+
+        def interleave(copy, grouped, source):
+            copy(
+                out=grouped.rearrange("p (c i) t -> p c t i", i=4),
+                in_=source.rearrange("p t (c i) -> p c t i", i=4),
+            )
+
+        def quantize(codes, scales, grouped):
+            nc.vector.quantize_mx(out=codes.bitcast(FP8X4), scales=scales, in_=grouped)
+
+        grouped_w = {}
+        quantised = {}
+
+        def cast(q, m, z, copy):
+            if q not in grouped_w:
+                grouped_w[q] = tile([P, 2, PASSES, P, PACK], BF16, "grouped_%d" % q)
+            staged = raw[("w2", "w1")[m], q]
+            if z == 2:
+                copy(
+                    out=grouped_w[q][:, m].rearrange("p z (c i) t -> p z c t i", i=4),
+                    in_=staged[:].rearrange("p (z t c i) -> p z c t i", z=PASSES, t=PACK, i=4),
+                )
+            else:
+                interleave(copy, grouped_w[q][:, m, z], staged[:, z * T : (z + 1) * T].rearrange("p (t c) -> p t c", t=PACK))
+
+        def quant(q, first, count):
+            if q not in quantised:
+                quantised[q] = (tile([P, 4 * P], U32, "codes_%d" % q), tile([P, 4 * P], U8, "scales_%d" % q))
+            codes, scales = quantised[q]
+            cols = slice(first * P, (first + count) * P)
+            flat = grouped_w[q][:].rearrange("p m z c t -> p (m z c t)")
+            quantize(codes[:, cols], scales[:, cols], flat[:, first * P * PACK : (first + count) * P * PACK])
+
+        accs = {}
+
+        def product(q, m):
+            codes, scales = quantised[q]
+            acc = products.tile([P, T], F32, name="acc")
+            for z in range(PASSES):
+                cols = slice((2 * m + z) * P, (2 * m + z + 1) * P)
+                nc.tensor.matmul_mx(
+                    out=acc[:],
+                    lhsT=codes[:, cols].bitcast(FP8X4),
+                    lhsT_scale=scales[:, cols],
+                    rhs=x_codes[z][:].bitcast(FP8X4),
+                    rhs_scale=x_planes[:, z, :],
+                    start=(z == 0),
+                    stop=(z == PASSES - 1),
+                )
+            accs[q, m] = acc
+
+        def empty(q, m):
+            if m == 1:
+                y_tiles[q] = slots[OPT["ytag"]] if q == 0 and OPT["ytag"] else tile([P, T], F32, "y_%d" % q)
+            nc.scalar.copy(out=y_tiles[q][:] if m else e_tiles[q][:, :T], in_=accs[q, m][:])
+
+        y_tiles = {}
+
+        picks = []
+
+        def edge(q, d, v0, width, act, tag=None):
+            n = len(picks)
+            where = OPT["tags"].split()[n]
+            if where == "-":
+                picked = tile([P, T], F32, "picked_%d" % n)[:]
+            elif where[0] == "p":
+                picked = picks[int(where[1:])]
+            else:
+                picked = slots[where]
+            picks.append(picked)
+            picked = picked[:, :width]
+            fused = 4 * q + d >= OPT["head"] and d >= OPT["dmin"]
+            window = e_tiles[q][:].indirect(lists[d][:, v0 // 16 : (v0 + width) // 16])
+            if fused:
+                nc.vector.tensor_tensor(picked[:], window, y_tiles[q][:, v0 : v0 + width], mybir.AluOpType.add)
+            else:
+                nc.vector.tensor_copy(out=picked[:], in_=window)
+            blocks = width // P
+            pre = edges.tile([P, T], F32, name="pre", tag="pre" if width >= OPT["tailw"] else "pre_tail", bufs=OPT["e"] if width >= OPT["tailw"] else OPT["et"])
+            for b in range(0 if fused else blocks):
+                nc.tensor.matmul(
+                    pre[:, b * P : (b + 1) * P],
+                    y_tiles[q][:, v0 + b * P : v0 + (b + 1) * P],
+                    identity[:],
+                    start=(b == 0),
+                    stop=False,
+                    is_transpose=True,
+                )
+            for b in range(blocks):
+                nc.tensor.matmul(
+                    pre[:, b * P : (b + 1) * P],
+                    picked[:, b * P : (b + 1) * P],
+                    identity[:],
+                    start=fused and b == 0,
+                    stop=(b == blocks - 1),
+                    is_transpose=True,
+                )
+            nc.scalar.activation(act, pre[:, :width], SILU)
+
+        z_rows = tile([P, T // P, H], BF16, "z_rows")
+
+        def larger_of_pairs(name, acts, width):
+            pairs = tile([P, 2 * width], BF16, "pairs_" + name)
+            nc.vector.tensor_tensor(pairs[:], acts[:, : 2 * width], acts[:, 2 * width :], MAX)
+            return pairs
+
+        def largest(q, v0, width, left, right):
+            nc.vector.tensor_tensor(
+                z_rows[:, v0 // P : (v0 + width) // P, q * P : (q + 1) * P],
+                left.rearrange("p (b i) -> p b i", i=P),
+                right.rearrange("p (b i) -> p b i", i=P),
+                MAX,
+            )
+
+        grouped_w3 = tile([P, N, PACK], BF16, "grouped_w3")
+        codes_w3 = tile([P, N], U32, "codes_w3")
+        scales_w3 = tile([P, N], U8, "scales_w3")
+        all_acts = {}
+        all_pairs = {}
+        for step in OPT["pre"].split():
+            kind = step[0]
+            n = [int(c) for c in step[1:]]
+            if kind == "c":
+                cast(n[0], n[1], n[2], nc.scalar.copy)
+            elif kind == "v":
+                cast(n[0], n[1], n[2], nc.vector.tensor_copy)
+            elif kind == "q":
+                quant(*n)
+            elif kind == "m":
+                product(*n)
+            elif kind == "e":
+                empty(*n)
+            elif kind == "w":
+                interleave(nc.scalar.copy, grouped_w3[:], raw_w3[:])
+            elif kind == "g":
+                q, d = n
+                if d == 0:
+                    all_acts[q] = tile([P, 4 * T], BF16, "acts_%d" % q)
+                edge(q, d, 0, T, all_acts[q][:, d * T : (d + 1) * T])
+            elif kind == "A":
+                all_pairs[n[0]] = larger_of_pairs(str(n[0]), all_acts[n[0]], T)
+            elif kind == "B":
+                largest(n[0], 0, T, all_pairs[n[0]][:, :T], all_pairs[n[0]][:, T:])
+        acts = all_acts[2]
+
+        q = TILES - 1
+
+        def turn(v0, width):
+            blocks = width // P
+            turned = products.tile([P, T], F32, name="acc")
+            for b in range(blocks):
+                words = z_rows[:, v0 // P + b, :].bitcast(F32)
+                for u in range(2):
+                    slot = 2 * b + u
+                    nc.tensor.transpose(turned[:, slot * P : (slot + 1) * P], words[:, u::2], identity[:])
+            grouped = tile([P, width * PACK], BF16, "grouped_z_%d" % v0)
+            nc.scalar.copy(
+                out=grouped[:].bitcast(F32).rearrange("p (b v u) -> p b v u", b=blocks, u=2),
+                in_=turned[:, : 2 * width].rearrange("p (b u v) -> p b v u", b=blocks, u=2),
+            )
+            return grouped
+
+        def project(v0, width, grouped):
+            codes = tile([P, width], U32, "codes_z_%d" % v0)
+            scales = tile([P, width], U8, "scales_z_%d" % v0)
+            quantize(codes[:], scales[:], grouped[:])
+            acc = products.tile([P, T], F32, name="acc")
+            nc.tensor.matmul_mx(
+                out=acc[:, :width],
+                lhsT=codes_w3[:].bitcast(FP8X4),
+                lhsT_scale=scales_w3[:],
+                rhs=codes[:].bitcast(FP8X4),
+                rhs_scale=scales[:],
+                start=True,
+                stop=True,
+            )
+            result = tile([P, width], F32, "result_%d" % v0)
+            nc.scalar.copy(out=result[:], in_=acc[:, :width])
+            nc.sync.dma_start(out=out[:, v0 : v0 + width], in_=result[:])
+
+        a0 = tile([P, 4 * 256], BF16, "acts_c0")
+        a1 = tile([P, 4 * P], BF16, "acts_c1")
+        a2 = tile([P, 4 * P], BF16, "acts_c2")
+
+        def part(acts, v0, width, d, tag=None):
+            edge(q, d, v0, width, acts[:, d * width : (d + 1) * width], tag)
+
+        part(a0, 0, 256, 0)
+        quantize(codes_w3[:], scales_w3[:], grouped_w3[:].rearrange("p c t -> p (c t)"))
+        part(a0, 0, 256, 1)
+        part(a0, 0, 256, 2)
+        pairs = larger_of_pairs("2", acts, T)
+        part(a0, 0, 256, 3)
+        largest(q - 1, 0, T, pairs[:, :T], pairs[:, T:])
+        part(a1, 256, P, 0)
+        part(a1, 256, P, 1)
+        part(a1, 256, P, 2)
+        pairs = larger_of_pairs("c0", a0, 256)
+        part(a1, 256, P, 3)
+        largest(q, 0, 256, pairs[:, :256], pairs[:, 256:])
+        g0 = turn(0, 256)
+        part(a2, 384, P, 0)
+        part(a2, 384, P, 1)
+        part(a2, 384, P, 2)
+        pairs = larger_of_pairs("c1", a1, P)
+        part(a2, 384, P, 3)
+        largest(q, 256, P, pairs[:, :P], pairs[:, P:])
+        g1 = turn(256, P)
+        project(0, 256, g0)
+        first = tile([P, P], BF16, "first")
+        nc.vector.tensor_tensor(first[:], a2[:, :P], a2[:, P : 2 * P], MAX)
+        second = tile([P, P], BF16, "second")
+        nc.vector.tensor_tensor(second[:], first[:], a2[:, 2 * P : 3 * P], MAX)
+        largest(q, 384, P, second[:], a2[:, 3 * P :])
+        g2 = turn(384, P)
+        project(256, P, g1)
+        project(384, P, g2)

@@ -26,15 +26,18 @@ CHUNK = 256
 OPT = {
  "head": 2,
  "dmin": 0,
- "sq": 1,
+ "sq": 0,
+ "split": 1,
  "e": 4,
  "et": 0,
  "tailw": 128,
- "prod": 3,
+ "prod": 4,
  "ytag": "y11",
+ "k": 4,
+ "k2": 4,
  "loads": "l0 y0 l1 e1 y1 l2 l3 e2 y2 e3 y3",
- "tags": "- e11 - - - y20 y21 y30 y31 w3 p5 p6 p7 p8 p9 p10 p13 p14 p15 p16 p17 p18 p19 p20",
- "pre": "v000 q001 v001 q011 m00 e00 v010 c011 q022 m01 c100 c101 q102 m10 c110 c111 q122 m11 e01 c200 e10 c201 e11 c212 q204 m20 m21 c302 c312 q304 w e20 e21 g00 g01 m30 e30 g02 m31 e31 g03 A0 B0 g10 g11 g12 g13 A1 B1 g20 g21 g22 g23"
+ "tags": "y00 e11 - - - e21 y21 e31 y31 y30 e30 y20 e20 e10 - y01",
+ "pre": "v000 q001 v001 q011 f v010 c011 q022 m01 c100 c101 q102 m10 c110 c111 q122 m11 e01 c202 q202 e10 e11 c212 q222 m20 m21 c302 q302 e20 c312 e21 q322 m30 m31 g00 g01 e30 g02 e31 g03 A0103 B0103 g10 g11 g12 g13 w x A1203 B1203 h020 h021 h022 h023 h030 h031 h032 h033 A2402 B2402 t0 h120 h121 h122 h123 h130 h131 h132 h133 A2423 B2423 t1 h220 h221 h222 h223 h230 h231 h232 h233 A0334 r1 B0334 r2 r3 p0 p1 t2 p2"
 }
 
 
@@ -81,9 +84,11 @@ def tile_picked_wedgecv_silu_l_kernel(
         x_codes = []
         for z in range(PASSES):
             words = tile([P, T], U32, "x_codes_%d" % z)
-            nc.sync.dma_start(
-                out=words[:].bitcast(I32), in_=x_words[z].rearrange("p n t -> p (n t)").bitcast(I32)
-            )
+            source = x_words[z].rearrange("p n t -> p (n t)").bitcast(I32)
+            pieces = 2 if z == 1 and OPT["split"] else 1
+            for h in range(pieces):
+                cols = slice(h * T // pieces, (h + 1) * T // pieces)
+                nc.sync.dma_start(out=words[:, cols].bitcast(I32), in_=source[:, cols])
             x_codes.append(words)
         for step in OPT["loads"].split():
             if step[0] == "l":
@@ -157,6 +162,24 @@ def tile_picked_wedgecv_silu_l_kernel(
                 )
             accs[q, m] = acc
 
+        def first_product():
+            codes, scales = quantised[0]
+            halves = [products.tile([P, T], F32, name="acc") for h in range(2)]
+            for z in range(PASSES):
+                for h in range(2):
+                    cols = slice(h * 256, (h + 1) * 256)
+                    nc.tensor.matmul_mx(
+                        out=halves[h][:, :256],
+                        lhsT=codes[:, z * P : (z + 1) * P].bitcast(FP8X4),
+                        lhsT_scale=scales[:, z * P : (z + 1) * P],
+                        rhs=x_codes[z][:, cols].bitcast(FP8X4),
+                        rhs_scale=x_planes[:, z, cols],
+                        start=(z == 0),
+                        stop=(z == PASSES - 1),
+                    )
+            nc.scalar.copy(out=e_tiles[0][:, :256], in_=halves[0][:, :256])
+            nc.vector.tensor_copy(out=e_tiles[0][:, 256:T], in_=halves[1][:, :256])
+
         def empty(q, m):
             if m == 1:
                 y_tiles[q] = slots[OPT["ytag"]] if q == 0 and OPT["ytag"] else tile([P, T], F32, "y_%d" % q)
@@ -168,7 +191,8 @@ def tile_picked_wedgecv_silu_l_kernel(
 
         def edge(q, d, v0, width, act, tag=None):
             n = len(picks)
-            where = OPT["tags"].split()[n]
+            tags = OPT["tags"].split()
+            where = tags[n] if n < len(tags) else "p%d" % (n - (OPT["k"] if width > P else OPT["k2"]))
             if where == "-":
                 picked = tile([P, T], F32, "picked_%d" % n)[:]
             elif where[0] == "p":
@@ -207,53 +231,37 @@ def tile_picked_wedgecv_silu_l_kernel(
 
         z_rows = tile([P, T // P, H], BF16, "z_rows")
 
-        def larger_of_pairs(name, acts, width):
-            pairs = tile([P, 2 * width], BF16, "pairs_" + name)
-            nc.vector.tensor_tensor(pairs[:], acts[:, : 2 * width], acts[:, 2 * width :], MAX)
-            return pairs
+        acts = tile([P, TILES * 4 * T], BF16, "acts")
+        acts_view = acts[:].rearrange("p (q d v) -> p q d v", q=TILES, d=4)
+        pairs = {}
 
-        def largest(q, v0, width, left, right):
+        def larger_of_pairs(name, q0, q1, v0, v1, where):
+            count = (q1 - q0) * 2 * (v1 - v0)
+            if where == "-":
+                target = tile([P, count], BF16, "pairs_" + name)[:]
+            else:
+                target = picks[int(where)].bitcast(BF16)[:, :count]
+            target = target.rearrange("p (q d v) -> p q d v", q=q1 - q0, d=2)
+            nc.vector.tensor_tensor(target, acts_view[:, q0:q1, 0:2, v0:v1], acts_view[:, q0:q1, 2:4, v0:v1], MAX)
+            pairs[name] = (q0, q1, v0, v1, target[:, :, 0], target[:, :, 1])
+
+        def largest(q0, q1, v0, v1, left, right):
             nc.vector.tensor_tensor(
-                z_rows[:, v0 // P : (v0 + width) // P, q * P : (q + 1) * P],
-                left.rearrange("p (b i) -> p b i", i=P),
-                right.rearrange("p (b i) -> p b i", i=P),
+                z_rows[:, v0 // P : v1 // P, q0 * P : q1 * P].rearrange("p b (q i) -> p q b i", i=P),
+                left.rearrange("p q (b i) -> p q b i", i=P),
+                right.rearrange("p q (b i) -> p q b i", i=P),
                 MAX,
             )
 
         grouped_w3 = tile([P, N, PACK], BF16, "grouped_w3")
         codes_w3 = tile([P, N], U32, "codes_w3")
         scales_w3 = tile([P, N], U8, "scales_w3")
-        all_acts = {}
-        all_pairs = {}
-        for step in OPT["pre"].split():
-            kind = step[0]
-            n = [int(c) for c in step[1:]]
-            if kind == "c":
-                cast(n[0], n[1], n[2], nc.scalar.copy)
-            elif kind == "v":
-                cast(n[0], n[1], n[2], nc.vector.tensor_copy)
-            elif kind == "q":
-                quant(*n)
-            elif kind == "m":
-                product(*n)
-            elif kind == "e":
-                empty(*n)
-            elif kind == "w":
-                interleave(nc.scalar.copy, grouped_w3[:], raw_w3[:])
-            elif kind == "g":
-                q, d = n
-                if d == 0:
-                    all_acts[q] = tile([P, 4 * T], BF16, "acts_%d" % q)
-                edge(q, d, 0, T, all_acts[q][:, d * T : (d + 1) * T])
-            elif kind == "A":
-                all_pairs[n[0]] = larger_of_pairs(str(n[0]), all_acts[n[0]], T)
-            elif kind == "B":
-                largest(n[0], 0, T, all_pairs[n[0]][:, :T], all_pairs[n[0]][:, T:])
-        acts = all_acts[2]
+        stretches = [(0, 256), (256, 384), (384, 512)]
+        grouped_z = {}
 
-        q = TILES - 1
-
-        def turn(v0, width):
+        def turn(c, copy):
+            v0, v1 = stretches[c]
+            width = v1 - v0
             blocks = width // P
             turned = products.tile([P, T], F32, name="acc")
             for b in range(blocks):
@@ -262,16 +270,18 @@ def tile_picked_wedgecv_silu_l_kernel(
                     slot = 2 * b + u
                     nc.tensor.transpose(turned[:, slot * P : (slot + 1) * P], words[:, u::2], identity[:])
             grouped = tile([P, width * PACK], BF16, "grouped_z_%d" % v0)
-            nc.scalar.copy(
+            copy(
                 out=grouped[:].bitcast(F32).rearrange("p (b v u) -> p b v u", b=blocks, u=2),
                 in_=turned[:, : 2 * width].rearrange("p (b u v) -> p b v u", b=blocks, u=2),
             )
-            return grouped
+            grouped_z[c] = grouped
 
-        def project(v0, width, grouped):
+        def project(c, copy):
+            v0, v1 = stretches[c]
+            width = v1 - v0
             codes = tile([P, width], U32, "codes_z_%d" % v0)
             scales = tile([P, width], U8, "scales_z_%d" % v0)
-            quantize(codes[:], scales[:], grouped[:])
+            quantize(codes[:], scales[:], grouped_z[c][:])
             acc = products.tile([P, T], F32, name="acc")
             nc.tensor.matmul_mx(
                 out=acc[:, :width],
@@ -283,43 +293,54 @@ def tile_picked_wedgecv_silu_l_kernel(
                 stop=True,
             )
             result = tile([P, width], F32, "result_%d" % v0)
-            nc.scalar.copy(out=result[:], in_=acc[:, :width])
-            nc.sync.dma_start(out=out[:, v0 : v0 + width], in_=result[:])
+            copy(out=result[:], in_=acc[:, :width])
+            nc.sync.dma_start(out=out[:, v0:v1], in_=result[:])
 
-        a0 = tile([P, 4 * 256], BF16, "acts_c0")
-        a1 = tile([P, 4 * P], BF16, "acts_c1")
-        a2 = tile([P, 4 * P], BF16, "acts_c2")
-
-        def part(acts, v0, width, d, tag=None):
-            edge(q, d, v0, width, acts[:, d * width : (d + 1) * width], tag)
-
-        part(a0, 0, 256, 0)
-        quantize(codes_w3[:], scales_w3[:], grouped_w3[:].rearrange("p c t -> p (c t)"))
-        part(a0, 0, 256, 1)
-        part(a0, 0, 256, 2)
-        pairs = larger_of_pairs("2", acts, T)
-        part(a0, 0, 256, 3)
-        largest(q - 1, 0, T, pairs[:, :T], pairs[:, T:])
-        part(a1, 256, P, 0)
-        part(a1, 256, P, 1)
-        part(a1, 256, P, 2)
-        pairs = larger_of_pairs("c0", a0, 256)
-        part(a1, 256, P, 3)
-        largest(q, 0, 256, pairs[:, :256], pairs[:, 256:])
-        g0 = turn(0, 256)
-        part(a2, 384, P, 0)
-        part(a2, 384, P, 1)
-        part(a2, 384, P, 2)
-        pairs = larger_of_pairs("c1", a1, P)
-        part(a2, 384, P, 3)
-        largest(q, 256, P, pairs[:, :P], pairs[:, P:])
-        g1 = turn(256, P)
-        project(0, 256, g0)
-        first = tile([P, P], BF16, "first")
-        nc.vector.tensor_tensor(first[:], a2[:, :P], a2[:, P : 2 * P], MAX)
-        second = tile([P, P], BF16, "second")
-        nc.vector.tensor_tensor(second[:], first[:], a2[:, 2 * P : 3 * P], MAX)
-        largest(q, 384, P, second[:], a2[:, 3 * P :])
-        g2 = turn(384, P)
-        project(256, P, g1)
-        project(384, P, g2)
+        running = {}
+        for step in OPT["pre"].split():
+            kind = step[0]
+            name, where = (step + ":").split(":")[:2]
+            n = [int(c) for c in name[1:]]
+            if kind == "c":
+                cast(n[0], n[1], n[2], nc.scalar.copy)
+            elif kind == "v":
+                cast(n[0], n[1], n[2], nc.vector.tensor_copy)
+            elif kind == "q":
+                quant(*n)
+            elif kind == "m":
+                product(*n)
+            elif kind == "f":
+                first_product()
+            elif kind == "e":
+                empty(*n)
+            elif kind == "w":
+                interleave(nc.scalar.copy, grouped_w3[:], raw_w3[:])
+            elif kind == "x":
+                quantize(codes_w3[:], scales_w3[:], grouped_w3[:].rearrange("p c t -> p (c t)"))
+            elif kind == "g":
+                q, d = n
+                edge(q, d, 0, T, acts_view[:, q, d, :])
+            elif kind == "h":
+                v0, v1 = stretches[n[0]]
+                edge(n[1], n[2], v0, v1 - v0, acts_view[:, n[1], n[2], v0:v1])
+            elif kind == "A":
+                larger_of_pairs(name[1:], n[0], n[1], n[2] * P, n[3] * P, where or "-")
+            elif kind == "B":
+                largest(*pairs[name[1:]])
+            elif kind == "r":
+                d = n[0]
+                left = acts_view[:, 3:4, 0, 384:T] if d == 1 else running[d - 1]
+                right = acts_view[:, 3:4, d, 384:T]
+                if d == 3:
+                    largest(3, 4, 384, T, left, right)
+                else:
+                    running[d] = tile([P, 1, P], BF16, "running_%d" % d)[:]
+                    nc.vector.tensor_tensor(running[d], left, right, MAX)
+            elif kind == "t":
+                turn(n[0], nc.scalar.copy)
+            elif kind == "T":
+                turn(n[0], nc.vector.tensor_copy)
+            elif kind == "p":
+                project(n[0], nc.scalar.copy)
+            elif kind == "P":
+                project(n[0], nc.vector.tensor_copy)

@@ -14,31 +14,19 @@ U16 = mybir.dt.uint16
 U8 = mybir.dt.uint8
 FP8X4 = mybir.dt.float8_e4m3fn_x4
 SILU = mybir.ActivationFunctionType.Silu
+ADD = mybir.AluOpType.add
 MAX = mybir.AluOpType.max
 
 P = 128
 PACK = 4
 PASSES = K // (P * PACK)
 TILES = H // P
+LISTS = 4
+HALF = T // 2
 WINDOW = 704
-CHUNK = 256
-
-OPT = {
- "head": 2,
- "dmin": 0,
- "sq": 0,
- "split": 1,
- "e": 4,
- "et": 0,
- "tailw": 128,
- "prod": 4,
- "ytag": "y11",
- "k": 4,
- "k2": 4,
- "loads": "l0 y0 l1 e1 y1 l2 l3 e2 y2 e3 y3",
- "tags": "y00 e11 - - - e21 y21 e31 y31 y30 e30 y20 e20 e10 - y01",
- "pre": "v000 q001 v001 q011 f v010 c011 q022 m01 c100 c101 q102 m10 c110 c111 q122 m11 e01 c202 q202 e10 e11 c212 q222 m20 m21 c302 q302 e20 c312 e21 q322 m30 m31 g00 g01 e30 g02 e31 g03 A0103 B0103 g10 g11 g12 g13 w x A1203 B1203 h020 h021 h022 h023 h030 h031 h032 h033 A2402 B2402 t0 h120 h121 h122 h123 h130 h131 h132 h133 A2423 B2423 t1 h220 h221 h222 h223 h230 h231 h232 h233 A0334 r1 B0334 r2 r3 p0 p1 t2 p2"
-}
+PLAIN_GATHERS = 6
+LAST_BLOCK_CAST_BY_PASS = 3
+BANKS = 4
 
 
 def tile_picked_wedgecv_silu_l_kernel(
@@ -47,31 +35,32 @@ def tile_picked_wedgecv_silu_l_kernel(
     nc = tc.nc
     with ExitStack() as ctx:
         held = ctx.enter_context(tc.tile_pool(name="held", bufs=1))
-        products = ctx.enter_context(tc.psum_pool(name="products", bufs=OPT["prod"]))
-        edges = ctx.enter_context(tc.psum_pool(name="edges", bufs=1))
+        products = ctx.enter_context(tc.psum_pool(name="products", bufs=BANKS))
+        sums = ctx.enter_context(tc.psum_pool(name="sums", bufs=BANKS))
 
-        def tile(shape, dtype, name, tag=None):
-            return held.tile(shape, dtype, name=name, tag=tag or name, align_bytes=64)
+        def tile(shape, dtype, name):
+            return held.tile(shape, dtype, name=name, align_bytes=64)
 
-        x_planes = tile([P, PASSES, T], U8, "x_planes")
-        nc.gpsimd.memset(x_planes[:].rearrange("p z c -> p (z c)").bitcast(I32), 0)
+        x_scale_rows = tile([P, PASSES, T], U8, "x_scale_rows")
+        nc.gpsimd.memset(x_scale_rows[:].rearrange("p g c -> p (g c)").bitcast(I32), 0)
         for quad in range(4):
-            (nc.scalar if OPT["sq"] else nc.sync).dma_start(
-                out=x_planes[32 * quad : 32 * quad + 4, :, :].bitcast(I32),
-                in_=x_scales[:, 4 * quad : 4 * quad + 4, :].rearrange("z r c -> r z c").bitcast(I32),
+            nc.sync.dma_start(
+                out=x_scale_rows[32 * quad : 32 * quad + 4, :, :].bitcast(I32),
+                in_=x_scales[:, 4 * quad : 4 * quad + 4, :].rearrange("g r c -> r g c").bitcast(I32),
             )
 
-        raw = {}
-        slots = {}
+        staged = []
 
-        def load_weight(name, w, first, count):
-            staged = tile([P, PASSES * PACK * P], F32, "raw_%s_%d" % (name, first))
-            for z in range(PASSES):
-                rows = w[z * P * PACK : (z + 1) * P * PACK, first * P : (first + 1) * P]
-                part = staged[:, z * T : (z + 1) * T]
-                nc.sync.dma_start(out=part.rearrange("p (j c) -> p j c", j=PACK), in_=rows.rearrange("(p j) c -> p j c", j=PACK))
-                slots["%s%d%d" % ({"w2": "e", "w1": "y"}[name], first, z)] = part
-            raw[name, first] = staged
+        def load_block():
+            q, is_w1 = divmod(len(staged), 2)
+            rows = tile([P, PASSES * T], F32, "staged_%d" % len(staged))
+            for g in range(PASSES):
+                source = (w1 if is_w1 else w2)[g * P * PACK : (g + 1) * P * PACK, q * P : (q + 1) * P]
+                nc.sync.dma_start(
+                    out=rows[:, g * T : (g + 1) * T].rearrange("p (t c) -> p t c", t=PACK),
+                    in_=source.rearrange("(p t) c -> p t c", t=PACK),
+                )
+            staged.append(rows)
 
         lists = []
 
@@ -80,267 +69,193 @@ def tile_picked_wedgecv_silu_l_kernel(
             nc.sync.dma_start(offsets[:], pos)
             lists.append(offsets)
 
-        load_weight("w2", w2, 0, 1)
-        x_codes = []
-        for z in range(PASSES):
-            words = tile([P, T], U32, "x_codes_%d" % z)
-            source = x_words[z].rearrange("p n t -> p (n t)").bitcast(I32)
-            pieces = 2 if z == 1 and OPT["split"] else 1
-            for h in range(pieces):
-                cols = slice(h * T // pieces, (h + 1) * T // pieces)
-                nc.sync.dma_start(out=words[:, cols].bitcast(I32), in_=source[:, cols])
-            x_codes.append(words)
-        for step in OPT["loads"].split():
-            if step[0] == "l":
-                load_list([pos1, pos2, pos3, pos4][int(step[1])])
-            elif step[0] == "e":
-                load_weight("w2", w2, int(step[1]), 1)
-            else:
-                load_weight("w1", w1, int(step[1]), 1)
-        raw_w3 = tile([P, PACK, N], F32, "raw_w3")
-        nc.sync.dma_start(out=raw_w3[:], in_=w3.rearrange("(p j) c -> p j c", j=PACK))
+        load_block()
+        x_codes = [tile([P, T], U32, "x_codes_%d" % g) for g in range(PASSES)]
+        x_source = [x_words[g].rearrange("p c t -> p (c t)").bitcast(I32) for g in range(PASSES)]
+        nc.sync.dma_start(out=x_codes[0][:].bitcast(I32), in_=x_source[0])
+        for v0 in (0, HALF):
+            nc.sync.dma_start(
+                out=x_codes[1][:, v0 : v0 + HALF].bitcast(I32), in_=x_source[1][:, v0 : v0 + HALF]
+            )
+        load_list(pos1)
+        load_list(pos2)
+        load_block()
+        load_list(pos3)
+        load_list(pos4)
+        while len(staged) < 2 * TILES:
+            load_block()
+        staged_w3 = tile([P, PACK, N], F32, "staged_w3")
+        nc.sync.dma_start(out=staged_w3[:], in_=w3.rearrange("(p t) c -> p t c", t=PACK))
 
-        e_tiles = []
-        for q in range(TILES):
-            e_sb = tile([P, WINDOW], F32, "e_%d" % q)
-            nc.gpsimd.memset(e_sb[:, T:], 0.0)
-            e_tiles.append(e_sb)
-
-        slots["w3"] = raw_w3[:].rearrange("p j c -> p (j c)")
+        e_tiles = [tile([P, WINDOW], F32, "e_%d" % q) for q in range(TILES)]
+        for q in range(1, TILES):
+            nc.gpsimd.memset(e_tiles[q][:, T:], 0.0)
+        nc.scalar.activation(e_tiles[0][:, T:], e_tiles[1][:, T:], SILU)
         identity = tile([P, P], F32, "identity")
         make_identity(nc, identity[:])
-        warm = tile([P, 1], F32, "warm")
-        nc.scalar.activation(warm[:], e_tiles[0][:, T : T + 1], SILU)
 
-        def interleave(copy, grouped, source):
+        def cast(copy, grouped, rows):
             copy(
-                out=grouped.rearrange("p (c i) t -> p c t i", i=4),
-                in_=source.rearrange("p t (c i) -> p c t i", i=4),
+                out=grouped.rearrange("p (g c i t) -> p g c t i", c=P // 4, i=4, t=PACK),
+                in_=rows.rearrange("p (g t c i) -> p g c t i", c=P // 4, i=4, t=PACK),
             )
 
-        def quantize(codes, scales, grouped):
-            nc.vector.quantize_mx(out=codes.bitcast(FP8X4), scales=scales, in_=grouped)
+        def quantize(name, grouped):
+            words = grouped.shape[1] // PACK
+            codes = tile([P, words], U32, "codes_" + name)
+            scales = tile([P, words], U8, "scales_" + name)
+            nc.vector.quantize_mx(out=codes[:].bitcast(FP8X4), scales=scales[:], in_=grouped)
+            return codes, scales
 
-        grouped_w = {}
-        quantised = {}
+        def matmul_mx(acc, lhs, lhs_cols, rhs_codes, rhs_scales, start, stop):
+            nc.tensor.matmul_mx(
+                out=acc,
+                lhsT=lhs[0][:, lhs_cols].bitcast(FP8X4),
+                lhsT_scale=lhs[1][:, lhs_cols],
+                rhs=rhs_codes.bitcast(FP8X4),
+                rhs_scale=rhs_scales,
+                start=start,
+                stop=stop,
+            )
 
-        def cast(q, m, z, copy):
-            if q not in grouped_w:
-                grouped_w[q] = tile([P, 2, PASSES, P, PACK], BF16, "grouped_%d" % q)
-            staged = raw[("w2", "w1")[m], q]
-            if z == 2:
-                copy(
-                    out=grouped_w[q][:, m].rearrange("p z (c i) t -> p z c t i", i=4),
-                    in_=staged[:].rearrange("p (z t c i) -> p z c t i", z=PASSES, t=PACK, i=4),
+        first_weights = []
+        for g in range(PASSES):
+            grouped = tile([P, T], BF16, "grouped_first_%d" % g)
+            cast(nc.vector.tensor_copy, grouped[:], staged[0][:, g * T : (g + 1) * T])
+            first_weights.append(quantize("first_%d" % g, grouped[:]))
+        halves = [products.tile([P, T], F32, name="acc") for v0 in (0, HALF)]
+        for g in range(PASSES):
+            for h, v0 in enumerate((0, HALF)):
+                cols = slice(v0, v0 + HALF)
+                matmul_mx(
+                    halves[h][:, :HALF], first_weights[g], slice(0, P),
+                    x_codes[g][:, cols], x_scale_rows[:, g, cols], g == 0, g == PASSES - 1,
                 )
-            else:
-                interleave(copy, grouped_w[q][:, m, z], staged[:, z * T : (z + 1) * T].rearrange("p (t c) -> p t c", t=PACK))
+        nc.scalar.copy(out=e_tiles[0][:, :HALF], in_=halves[0][:, :HALF])
+        nc.vector.tensor_copy(out=e_tiles[0][:, HALF:T], in_=halves[1][:, :HALF])
 
-        def quant(q, first, count):
-            if q not in quantised:
-                quantised[q] = (tile([P, 4 * P], U32, "codes_%d" % q), tile([P, 4 * P], U8, "scales_%d" % q))
-            codes, scales = quantised[q]
-            cols = slice(first * P, (first + count) * P)
-            flat = grouped_w[q][:].rearrange("p m z c t -> p (m z c t)")
-            quantize(codes[:, cols], scales[:, cols], flat[:, first * P * PACK : (first + count) * P * PACK])
-
+        y_tiles = [staged[q + 3][:, :T] for q in range(TILES)]
         accs = {}
 
-        def product(q, m):
-            codes, scales = quantised[q]
-            acc = products.tile([P, T], F32, name="acc")
-            for z in range(PASSES):
-                cols = slice((2 * m + z) * P, (2 * m + z + 1) * P)
-                nc.tensor.matmul_mx(
-                    out=acc[:],
-                    lhsT=codes[:, cols].bitcast(FP8X4),
-                    lhsT_scale=scales[:, cols],
-                    rhs=x_codes[z][:].bitcast(FP8X4),
-                    rhs_scale=x_planes[:, z, :],
-                    start=(z == 0),
-                    stop=(z == PASSES - 1),
-                )
-            accs[q, m] = acc
-
-        def first_product():
-            codes, scales = quantised[0]
-            halves = [products.tile([P, T], F32, name="acc") for h in range(2)]
-            for z in range(PASSES):
-                for h in range(2):
-                    cols = slice(h * 256, (h + 1) * 256)
-                    nc.tensor.matmul_mx(
-                        out=halves[h][:, :256],
-                        lhsT=codes[:, z * P : (z + 1) * P].bitcast(FP8X4),
-                        lhsT_scale=scales[:, z * P : (z + 1) * P],
-                        rhs=x_codes[z][:, cols].bitcast(FP8X4),
-                        rhs_scale=x_planes[:, z, cols],
-                        start=(z == 0),
-                        stop=(z == PASSES - 1),
-                    )
-            nc.scalar.copy(out=e_tiles[0][:, :256], in_=halves[0][:, :256])
-            nc.vector.tensor_copy(out=e_tiles[0][:, 256:T], in_=halves[1][:, :256])
-
-        def empty(q, m):
-            if m == 1:
-                y_tiles[q] = slots[OPT["ytag"]] if q == 0 and OPT["ytag"] else tile([P, T], F32, "y_%d" % q)
-            nc.scalar.copy(out=y_tiles[q][:] if m else e_tiles[q][:, :T], in_=accs[q, m][:])
-
-        y_tiles = {}
-
-        picks = []
-
-        def edge(q, d, v0, width, act, tag=None):
-            n = len(picks)
-            tags = OPT["tags"].split()
-            where = tags[n] if n < len(tags) else "p%d" % (n - (OPT["k"] if width > P else OPT["k2"]))
-            if where == "-":
-                picked = tile([P, T], F32, "picked_%d" % n)[:]
-            elif where[0] == "p":
-                picked = picks[int(where[1:])]
+        def product(b):
+            grouped = tile([P, PASSES * T], BF16, "grouped_%d" % b)
+            if b <= LAST_BLOCK_CAST_BY_PASS:
+                for g in range(PASSES):
+                    cols = slice(g * T, (g + 1) * T)
+                    cast(nc.scalar.copy, grouped[:, cols], staged[b][:, cols])
             else:
-                picked = slots[where]
-            picks.append(picked)
-            picked = picked[:, :width]
-            fused = 4 * q + d >= OPT["head"] and d >= OPT["dmin"]
+                cast(nc.scalar.copy, grouped[:], staged[b][:])
+            weights = quantize(str(b), grouped[:])
+            accs[b] = products.tile([P, T], F32, name="acc")
+            for g in range(PASSES):
+                matmul_mx(
+                    accs[b][:], weights, slice(g * P, (g + 1) * P),
+                    x_codes[g][:], x_scale_rows[:, g, :], g == 0, g == PASSES - 1,
+                )
+
+        def empty(b):
+            q, is_w1 = divmod(b, 2)
+            nc.scalar.copy(out=y_tiles[q] if is_w1 else e_tiles[q][:, :T], in_=accs[b][:])
+
+        for b in range(1, 2 * TILES):
+            product(b)
+            if b >= 3:
+                empty(b - 2)
+
+        acts = tile([P, TILES * LISTS * T], BF16, "acts")
+        acts_view = acts[:].rearrange("p (q d v) -> p q d v", q=TILES, d=LISTS)
+
+        staging_for = dict(zip((1, 2, 3, 5, 6, 7, 8), range(1, 2 * TILES)))
+        first_reusing = 14
+        gathered = []
+
+        def edge(q, d, v0, width):
+            n = len(gathered)
+            if n in staging_for:
+                rows = staged[staging_for[n]][:, T:]
+            elif n >= first_reusing:
+                rows = gathered[n - BANKS]
+            else:
+                rows = tile([P, T], F32, "gathered_%d" % n)[:]
+            gathered.append(rows)
+            picked = rows[:, :width]
             window = e_tiles[q][:].indirect(lists[d][:, v0 // 16 : (v0 + width) // 16])
-            if fused:
-                nc.vector.tensor_tensor(picked[:], window, y_tiles[q][:, v0 : v0 + width], mybir.AluOpType.add)
+            y_part = y_tiles[q][:, v0 : v0 + width]
+            if n < PLAIN_GATHERS:
+                nc.vector.tensor_copy(out=picked, in_=window)
+                terms = [y_part, picked]
             else:
-                nc.vector.tensor_copy(out=picked[:], in_=window)
+                nc.vector.tensor_tensor(picked, window, y_part, ADD)
+                terms = [picked]
+            bank = sums.tile([P, T], F32, name="bank")
             blocks = width // P
-            pre = edges.tile([P, T], F32, name="pre", tag="pre" if width >= OPT["tailw"] else "pre_tail", bufs=OPT["e"] if width >= OPT["tailw"] else OPT["et"])
-            for b in range(0 if fused else blocks):
-                nc.tensor.matmul(
-                    pre[:, b * P : (b + 1) * P],
-                    y_tiles[q][:, v0 + b * P : v0 + (b + 1) * P],
-                    identity[:],
-                    start=(b == 0),
-                    stop=False,
-                    is_transpose=True,
-                )
-            for b in range(blocks):
-                nc.tensor.matmul(
-                    pre[:, b * P : (b + 1) * P],
-                    picked[:, b * P : (b + 1) * P],
-                    identity[:],
-                    start=fused and b == 0,
-                    stop=(b == blocks - 1),
-                    is_transpose=True,
-                )
-            nc.scalar.activation(act, pre[:, :width], SILU)
+            for j, term in enumerate(terms):
+                for block in range(blocks):
+                    cols = slice(block * P, (block + 1) * P)
+                    nc.tensor.matmul(
+                        bank[:, cols], term[:, cols], identity[:], is_transpose=True,
+                        start=(j == 0 and block == 0),
+                        stop=(j == len(terms) - 1 and block == blocks - 1),
+                    )
+            nc.scalar.activation(acts_view[:, q, d, v0 : v0 + width], bank[:, :width], SILU)
 
         z_rows = tile([P, T // P, H], BF16, "z_rows")
 
-        acts = tile([P, TILES * 4 * T], BF16, "acts")
-        acts_view = acts[:].rearrange("p (q d v) -> p q d v", q=TILES, d=4)
-        pairs = {}
-
-        def larger_of_pairs(name, q0, q1, v0, v1, where):
-            count = (q1 - q0) * 2 * (v1 - v0)
-            if where == "-":
-                target = tile([P, count], BF16, "pairs_" + name)[:]
-            else:
-                target = picks[int(where)].bitcast(BF16)[:, :count]
-            target = target.rearrange("p (q d v) -> p q d v", q=q1 - q0, d=2)
-            nc.vector.tensor_tensor(target, acts_view[:, q0:q1, 0:2, v0:v1], acts_view[:, q0:q1, 2:4, v0:v1], MAX)
-            pairs[name] = (q0, q1, v0, v1, target[:, :, 0], target[:, :, 1])
-
-        def largest(q0, q1, v0, v1, left, right):
+        def largest_into_z(q0, v0, width, left, right):
             nc.vector.tensor_tensor(
-                z_rows[:, v0 // P : v1 // P, q0 * P : q1 * P].rearrange("p b (q i) -> p q b i", i=P),
-                left.rearrange("p q (b i) -> p q b i", i=P),
-                right.rearrange("p q (b i) -> p q b i", i=P),
+                z_rows[:, v0 // P : (v0 + width) // P, q0 * P : (q0 + 2) * P].rearrange(
+                    "p b (q c) -> p q b c", c=P
+                ),
+                left.rearrange("p q (b c) -> p q b c", c=P),
+                right.rearrange("p q (b c) -> p q b c", c=P),
                 MAX,
             )
 
-        grouped_w3 = tile([P, N, PACK], BF16, "grouped_w3")
-        codes_w3 = tile([P, N], U32, "codes_w3")
-        scales_w3 = tile([P, N], U8, "scales_w3")
-        stretches = [(0, 256), (256, 384), (384, 512)]
-        grouped_z = {}
+        for d in range(LISTS):
+            edge(0, d, 0, T)
+            if d % 2 == 1:
+                empty(2 * TILES - 2 + d // 2)
+        for d in range(LISTS):
+            edge(1, d, 0, T)
+        pairs = tile([P, 2, 2, T], BF16, "pairs")
+        nc.vector.tensor_tensor(pairs[:], acts_view[:, 0:2, 0:2, :], acts_view[:, 0:2, 2:4, :], MAX)
+        largest_into_z(0, 0, T, pairs[:, :, 0, :], pairs[:, :, 1, :])
+        for d in range(LISTS):
+            edge(2, d, 0, T)
+        for d in range(LISTS - 1):
+            edge(3, d, 0, T)
+        grouped_w3 = tile([P, N * PACK], BF16, "grouped_w3")
+        cast(nc.scalar.copy, grouped_w3[:], staged_w3[:].rearrange("p t c -> p (t c)"))
+        for v0 in (0, HALF):
+            edge(3, LISTS - 1, v0, HALF)
 
-        def turn(c, copy):
-            v0, v1 = stretches[c]
-            width = v1 - v0
-            blocks = width // P
+        running = acts_view[:, 2:4, 0, :]
+        for d in range(1, LISTS - 1):
+            larger = tile([P, 2, T], BF16, "larger_%d" % d)
+            for v0 in (0, HALF):
+                cols = slice(v0, v0 + HALF)
+                nc.vector.tensor_tensor(larger[:, :, cols], running[:, :, cols], acts_view[:, 2:4, d, cols], MAX)
+            running = larger[:]
+        weights_w3 = quantize("w3", grouped_w3[:])
+
+        grouped_z = []
+        for block in range(T // P):
+            cols = slice(block * P, (block + 1) * P)
+            largest_into_z(2, block * P, P, running[:, :, cols], acts_view[:, 2:4, LISTS - 1, cols])
+            words = z_rows[:, block, :].bitcast(F32)
             turned = products.tile([P, T], F32, name="acc")
-            for b in range(blocks):
-                words = z_rows[:, v0 // P + b, :].bitcast(F32)
-                for u in range(2):
-                    slot = 2 * b + u
-                    nc.tensor.transpose(turned[:, slot * P : (slot + 1) * P], words[:, u::2], identity[:])
-            grouped = tile([P, width * PACK], BF16, "grouped_z_%d" % v0)
-            copy(
-                out=grouped[:].bitcast(F32).rearrange("p (b v u) -> p b v u", b=blocks, u=2),
-                in_=turned[:, : 2 * width].rearrange("p (b u v) -> p b v u", b=blocks, u=2),
+            for u in range(2):
+                nc.tensor.transpose(turned[:, u * P : (u + 1) * P], words[:, u::2], identity[:])
+            grouped = tile([P, P * PACK], BF16, "grouped_z_%d" % block)
+            nc.scalar.copy(
+                out=grouped[:].bitcast(F32).rearrange("p (v u) -> p v u", u=2),
+                in_=turned[:, : 2 * P].rearrange("p (u v) -> p v u", u=2),
             )
-            grouped_z[c] = grouped
-
-        def project(c, copy):
-            v0, v1 = stretches[c]
-            width = v1 - v0
-            codes = tile([P, width], U32, "codes_z_%d" % v0)
-            scales = tile([P, width], U8, "scales_z_%d" % v0)
-            quantize(codes[:], scales[:], grouped_z[c][:])
+            grouped_z.append(grouped)
+        for block in range(T // P):
+            codes, scales = quantize("z_%d" % block, grouped_z[block][:])
             acc = products.tile([P, T], F32, name="acc")
-            nc.tensor.matmul_mx(
-                out=acc[:, :width],
-                lhsT=codes_w3[:].bitcast(FP8X4),
-                lhsT_scale=scales_w3[:],
-                rhs=codes[:].bitcast(FP8X4),
-                rhs_scale=scales[:],
-                start=True,
-                stop=True,
-            )
-            result = tile([P, width], F32, "result_%d" % v0)
-            copy(out=result[:], in_=acc[:, :width])
-            nc.sync.dma_start(out=out[:, v0:v1], in_=result[:])
-
-        running = {}
-        for step in OPT["pre"].split():
-            kind = step[0]
-            name, where = (step + ":").split(":")[:2]
-            n = [int(c) for c in name[1:]]
-            if kind == "c":
-                cast(n[0], n[1], n[2], nc.scalar.copy)
-            elif kind == "v":
-                cast(n[0], n[1], n[2], nc.vector.tensor_copy)
-            elif kind == "q":
-                quant(*n)
-            elif kind == "m":
-                product(*n)
-            elif kind == "f":
-                first_product()
-            elif kind == "e":
-                empty(*n)
-            elif kind == "w":
-                interleave(nc.scalar.copy, grouped_w3[:], raw_w3[:])
-            elif kind == "x":
-                quantize(codes_w3[:], scales_w3[:], grouped_w3[:].rearrange("p c t -> p (c t)"))
-            elif kind == "g":
-                q, d = n
-                edge(q, d, 0, T, acts_view[:, q, d, :])
-            elif kind == "h":
-                v0, v1 = stretches[n[0]]
-                edge(n[1], n[2], v0, v1 - v0, acts_view[:, n[1], n[2], v0:v1])
-            elif kind == "A":
-                larger_of_pairs(name[1:], n[0], n[1], n[2] * P, n[3] * P, where or "-")
-            elif kind == "B":
-                largest(*pairs[name[1:]])
-            elif kind == "r":
-                d = n[0]
-                left = acts_view[:, 3:4, 0, 384:T] if d == 1 else running[d - 1]
-                right = acts_view[:, 3:4, d, 384:T]
-                if d == 3:
-                    largest(3, 4, 384, T, left, right)
-                else:
-                    running[d] = tile([P, 1, P], BF16, "running_%d" % d)[:]
-                    nc.vector.tensor_tensor(running[d], left, right, MAX)
-            elif kind == "t":
-                turn(n[0], nc.scalar.copy)
-            elif kind == "T":
-                turn(n[0], nc.vector.tensor_copy)
-            elif kind == "p":
-                project(n[0], nc.scalar.copy)
-            elif kind == "P":
-                project(n[0], nc.vector.tensor_copy)
+            matmul_mx(acc[:, :P], weights_w3, slice(0, N), codes[:], scales[:], True, True)
+            result = tile([P, P], F32, "result_%d" % block)
+            nc.scalar.copy(out=result[:], in_=acc[:, :P])
+            nc.sync.dma_start(out=out[:, block * P : (block + 1) * P], in_=result[:])

@@ -24,7 +24,7 @@ TILES = H // P
 LISTS = 4
 HALF = T // 2
 WINDOW = 704
-PLAIN_GATHERS = 6
+PLAIN_LISTS = 2
 LAST_BLOCK_CAST_BY_PASS = 3
 BANKS = 4
 
@@ -71,12 +71,9 @@ def tile_picked_wedgecv_silu_l_kernel(
 
         load_block()
         x_codes = [tile([P, T], U32, "x_codes_%d" % g) for g in range(PASSES)]
-        x_source = [x_words[g].rearrange("p c t -> p (c t)").bitcast(I32) for g in range(PASSES)]
-        nc.sync.dma_start(out=x_codes[0][:].bitcast(I32), in_=x_source[0])
-        for v0 in (0, HALF):
-            nc.sync.dma_start(
-                out=x_codes[1][:, v0 : v0 + HALF].bitcast(I32), in_=x_source[1][:, v0 : v0 + HALF]
-            )
+        for g in range(PASSES):
+            source = x_words[g].rearrange("p c t -> p (c t)").bitcast(I32)
+            nc.sync.dma_start(out=x_codes[g][:].bitcast(I32), in_=source)
         load_list(pos1)
         load_list(pos2)
         load_block()
@@ -181,7 +178,7 @@ def tile_picked_wedgecv_silu_l_kernel(
             picked = rows[:, :width]
             window = e_tiles[q][:].indirect(lists[d][:, v0 // 16 : (v0 + width) // 16])
             y_part = y_tiles[q][:, v0 : v0 + width]
-            if n < PLAIN_GATHERS:
+            if q == 0 or d < PLAIN_LISTS:
                 nc.vector.tensor_copy(out=picked, in_=window)
                 terms = [y_part, picked]
             else:
@@ -224,10 +221,10 @@ def tile_picked_wedgecv_silu_l_kernel(
             edge(2, d, 0, T)
         for d in range(LISTS - 1):
             edge(3, d, 0, T)
-        grouped_w3 = tile([P, N * PACK], BF16, "grouped_w3")
-        cast(nc.scalar.copy, grouped_w3[:], staged_w3[:].rearrange("p t c -> p (t c)"))
         for v0 in (0, HALF):
             edge(3, LISTS - 1, v0, HALF)
+        grouped_w3 = tile([P, N * PACK], BF16, "grouped_w3")
+        cast(nc.scalar.copy, grouped_w3[:], staged_w3[:].rearrange("p t c -> p (t c)"))
 
         running = acts_view[:, 2:4, 0, :]
         for d in range(1, LISTS - 1):
@@ -236,7 +233,6 @@ def tile_picked_wedgecv_silu_l_kernel(
                 cols = slice(v0, v0 + HALF)
                 nc.vector.tensor_tensor(larger[:, :, cols], running[:, :, cols], acts_view[:, 2:4, d, cols], MAX)
             running = larger[:]
-        weights_w3 = quantize("w3", grouped_w3[:])
 
         grouped_z = []
         for block in range(T // P):
@@ -252,6 +248,7 @@ def tile_picked_wedgecv_silu_l_kernel(
                 in_=turned[:, : 2 * P].rearrange("p (u v) -> p v u", u=2),
             )
             grouped_z.append(grouped)
+        weights_w3 = quantize("w3", grouped_w3[:])
         for block in range(T // P):
             codes, scales = quantize("z_%d" % block, grouped_z[block][:])
             acc = products.tile([P, T], F32, name="acc")

@@ -24,7 +24,7 @@ TILES = H // P
 LISTS = 4
 HALF = T // 2
 WINDOW = 704
-PLAIN_LISTS = 2
+PLAIN_GATHERS = 6
 LAST_BLOCK_CAST_BY_PASS = 3
 BANKS = 4
 
@@ -159,14 +159,14 @@ def tile_picked_wedgecv_silu_l_kernel(
             if b >= 3:
                 empty(b - 2)
 
-        acts = tile([P, TILES * LISTS * T], BF16, "acts")
-        acts_view = acts[:].rearrange("p (q d v) -> p q d v", q=TILES, d=LISTS)
+        acts = tile([P, TILES, LISTS, 2, 2, P], BF16, "acts")
+        last = tile([P, 2, 2, 2, P], BF16, "last")
 
         staging_for = dict(zip((1, 2, 3, 5, 6, 7, 8), range(1, 2 * TILES)))
         first_reusing = 14
         gathered = []
 
-        def edge(q, d, v0, width):
+        def edge(q, d, v0, width, target):
             n = len(gathered)
             if n in staging_for:
                 rows = staged[staging_for[n]][:, T:]
@@ -178,7 +178,7 @@ def tile_picked_wedgecv_silu_l_kernel(
             picked = rows[:, :width]
             window = e_tiles[q][:].indirect(lists[d][:, v0 // 16 : (v0 + width) // 16])
             y_part = y_tiles[q][:, v0 : v0 + width]
-            if q == 0 or d < PLAIN_LISTS:
+            if n < PLAIN_GATHERS:
                 nc.vector.tensor_copy(out=picked, in_=window)
                 terms = [y_part, picked]
             else:
@@ -194,54 +194,57 @@ def tile_picked_wedgecv_silu_l_kernel(
                         start=(j == 0 and block == 0),
                         stop=(j == len(terms) - 1 and block == blocks - 1),
                     )
-            nc.scalar.activation(acts_view[:, q, d, v0 : v0 + width], bank[:, :width], SILU)
+            nc.scalar.activation(
+                target.rearrange("p u h (m j) -> p u h m j", j=2),
+                bank[:, :width].rearrange("p (h m u j) -> p u h m j", m=P // 2, u=2, j=2),
+                SILU,
+            )
 
-        z_rows = tile([P, T // P, H], BF16, "z_rows")
+        z_rows = [tile([P, 2, TILES, P // 2], BF16, "z_rows_%d" % block) for block in range(T // P)]
 
-        def largest_into_z(q0, v0, width, left, right):
+        def largest_into_z(block, q0, left, right):
+            part = slice(block % 2 * (P // 2), (block % 2 + 1) * (P // 2))
             nc.vector.tensor_tensor(
-                z_rows[:, v0 // P : (v0 + width) // P, q0 * P : (q0 + 2) * P].rearrange(
-                    "p b (q c) -> p q b c", c=P
-                ),
-                left.rearrange("p q (b c) -> p q b c", c=P),
-                right.rearrange("p q (b c) -> p q b c", c=P),
+                z_rows[block][:, :, q0 : q0 + 2, :].rearrange("p u q y -> p q u y"),
+                left[:, :, :, part],
+                right[:, :, :, part],
                 MAX,
             )
 
         for d in range(LISTS):
-            edge(0, d, 0, T)
+            edge(0, d, 0, T, acts[:, 0, d])
             if d % 2 == 1:
                 empty(2 * TILES - 2 + d // 2)
         for d in range(LISTS):
-            edge(1, d, 0, T)
-        pairs = tile([P, 2, 2, T], BF16, "pairs")
-        nc.vector.tensor_tensor(pairs[:], acts_view[:, 0:2, 0:2, :], acts_view[:, 0:2, 2:4, :], MAX)
-        largest_into_z(0, 0, T, pairs[:, :, 0, :], pairs[:, :, 1, :])
-        for d in range(LISTS):
-            edge(2, d, 0, T)
-        for d in range(LISTS - 1):
-            edge(3, d, 0, T)
-        for v0 in (0, HALF):
-            edge(3, LISTS - 1, v0, HALF)
+            edge(1, d, 0, T, acts[:, 1, d])
+        pairs = tile([P, 2, 2, 2, 2, P], BF16, "pairs")
+        nc.vector.tensor_tensor(pairs[:], acts[:, 0:2, 0:2], acts[:, 0:2, 2:4], MAX)
+        for block in range(T // P):
+            largest_into_z(block, 0, pairs[:, :, 0, :, block // 2], pairs[:, :, 1, :, block // 2])
+        for q in (2, 3):
+            for d in range(LISTS - 1):
+                edge(q, d, 0, T, acts[:, q, d])
+            if q == 2:
+                edge(q, LISTS - 1, 0, T, last[:, :, 0].rearrange("p h u x -> p u h x"))
+        for h in range(2):
+            edge(3, LISTS - 1, h * HALF, HALF, last[:, h : h + 1, 1].rearrange("p h u x -> p u h x"))
         grouped_w3 = tile([P, N * PACK], BF16, "grouped_w3")
         cast(nc.scalar.copy, grouped_w3[:], staged_w3[:].rearrange("p t c -> p (t c)"))
 
-        running = acts_view[:, 2:4, 0, :]
+        running = [acts[:, 2:4, 0, :, h] for h in range(2)]
         for d in range(1, LISTS - 1):
-            larger = tile([P, 2, T], BF16, "larger_%d" % d)
-            for v0 in (0, HALF):
-                cols = slice(v0, v0 + HALF)
-                nc.vector.tensor_tensor(larger[:, :, cols], running[:, :, cols], acts_view[:, 2:4, d, cols], MAX)
-            running = larger[:]
+            for h in range(2):
+                larger = tile([P, 2, 2, P], BF16, "larger_%d_%d" % (d, h))
+                nc.vector.tensor_tensor(larger[:], running[h], acts[:, 2:4, d, :, h], MAX)
+                running[h] = larger[:]
 
         grouped_z = []
         for block in range(T // P):
-            cols = slice(block * P, (block + 1) * P)
-            largest_into_z(2, block * P, P, running[:, :, cols], acts_view[:, 2:4, LISTS - 1, cols])
-            words = z_rows[:, block, :].bitcast(F32)
+            largest_into_z(block, 2, running[block // 2], last[:, block // 2])
             turned = products.tile([P, T], F32, name="acc")
             for u in range(2):
-                nc.tensor.transpose(turned[:, u * P : (u + 1) * P], words[:, u::2], identity[:])
+                words = z_rows[block][:, u].rearrange("p q y -> p (q y)").bitcast(F32)
+                nc.tensor.transpose(turned[:, u * P : (u + 1) * P], words, identity[:])
             grouped = tile([P, P * PACK], BF16, "grouped_z_%d" % block)
             nc.scalar.copy(
                 out=grouped[:].bitcast(F32).rearrange("p (v u) -> p v u", u=2),

from contextlib import ExitStack

import concourse.mybir as mybir
from concourse.masks import make_identity

K, T, H, N = 1024, 512, 512, 128
FLOPS = 2 * (2 * K * H * T + H * N * T)

F32 = mybir.dt.float32
BF16 = mybir.dt.bfloat16
I32 = mybir.dt.int32
U32 = mybir.dt.uint32
U16 = mybir.dt.uint16
U8 = mybir.dt.uint8
FP8X4 = mybir.dt.float8_e4m3fn_x4
SILU = mybir.ActivationFunctionType.Silu
ADD = mybir.AluOpType.add
MAX = mybir.AluOpType.max

P = 128
PACK = 4
PASSES = K // (P * PACK)
TILES = H // P
LISTS = 4
HALF = T // 2
WINDOW = 704
PLAIN_GATHERS = 6
LAST_BLOCK_CAST_BY_PASS = 3
BANKS = 4


def tile_picked_wedgecv_silu_l_kernel(
    tc, x_words, x_scales, w1, w2, w3, pos1, pos2, pos3, pos4, out
):
    nc = tc.nc
    with ExitStack() as ctx:
        held = ctx.enter_context(tc.tile_pool(name="held", bufs=1))
        products = ctx.enter_context(tc.psum_pool(name="products", bufs=BANKS))
        sums = ctx.enter_context(tc.psum_pool(name="sums", bufs=BANKS))

        def tile(shape, dtype, name):
            return held.tile(shape, dtype, name=name, align_bytes=64)

        x_scale_rows = tile([P, PASSES, T], U8, "x_scale_rows")
        nc.gpsimd.memset(x_scale_rows[:].rearrange("p g c -> p (g c)").bitcast(I32), 0)
        for quad in range(4):
            nc.sync.dma_start(
                out=x_scale_rows[32 * quad : 32 * quad + 4, :, :].bitcast(I32),
                in_=x_scales[:, 4 * quad : 4 * quad + 4, :].rearrange("g r c -> r g c").bitcast(I32),
            )

        staged = []

        def load_block():
            q, is_w1 = divmod(len(staged), 2)
            rows = tile([P, PASSES * T], F32, "staged_%d" % len(staged))
            for g in range(PASSES):
                source = (w1 if is_w1 else w2)[g * P * PACK : (g + 1) * P * PACK, q * P : (q + 1) * P]
                nc.sync.dma_start(
                    out=rows[:, g * T : (g + 1) * T].rearrange("p (t c) -> p t c", t=PACK),
                    in_=source.rearrange("(p t) c -> p t c", t=PACK),
                )
            staged.append(rows)

        lists = []

        def load_list(pos):
            offsets = held.tile([P, T // 16], U16, name="list_%d" % len(lists))
            nc.sync.dma_start(offsets[:], pos)
            lists.append(offsets)

        load_block()
        x_codes = [tile([P, T], U32, "x_codes_%d" % g) for g in range(PASSES)]
        for g in range(PASSES):
            source = x_words[g].rearrange("p c t -> p (c t)").bitcast(I32)
            nc.sync.dma_start(out=x_codes[g][:].bitcast(I32), in_=source)
        load_list(pos1)
        load_list(pos2)
        load_block()
        load_list(pos3)
        load_list(pos4)
        while len(staged) < 2 * TILES:
            load_block()
        staged_w3 = tile([P, PACK, N], F32, "staged_w3")
        nc.sync.dma_start(out=staged_w3[:], in_=w3.rearrange("(p t) c -> p t c", t=PACK))

        e_tiles = [tile([P, WINDOW], F32, "e_%d" % q) for q in range(TILES)]
        for q in range(1, TILES):
            nc.gpsimd.memset(e_tiles[q][:, T:], 0.0)
        nc.scalar.activation(e_tiles[0][:, T:], e_tiles[1][:, T:], SILU)
        identity = tile([P, P], F32, "identity")
        make_identity(nc, identity[:])

        def cast(copy, grouped, rows):
            copy(
                out=grouped.rearrange("p (g c i t) -> p g c t i", c=P // 4, i=4, t=PACK),
                in_=rows.rearrange("p (g t c i) -> p g c t i", c=P // 4, i=4, t=PACK),
            )

        def quantize(name, grouped):
            words = grouped.shape[1] // PACK
            codes = tile([P, words], U32, "codes_" + name)
            scales = tile([P, words], U8, "scales_" + name)
            nc.vector.quantize_mx(out=codes[:].bitcast(FP8X4), scales=scales[:], in_=grouped)
            return codes, scales

        def matmul_mx(acc, lhs, lhs_cols, rhs_codes, rhs_scales, start, stop):
            nc.tensor.matmul_mx(
                out=acc,
                lhsT=lhs[0][:, lhs_cols].bitcast(FP8X4),
                lhsT_scale=lhs[1][:, lhs_cols],
                rhs=rhs_codes.bitcast(FP8X4),
                rhs_scale=rhs_scales,
                start=start,
                stop=stop,
            )

        first_weights = []
        for g in range(PASSES):
            grouped = tile([P, T], BF16, "grouped_first_%d" % g)
            cast(nc.vector.tensor_copy, grouped[:], staged[0][:, g * T : (g + 1) * T])
            first_weights.append(quantize("first_%d" % g, grouped[:]))
        halves = [products.tile([P, T], F32, name="acc") for v0 in (0, HALF)]
        for g in range(PASSES):
            for h, v0 in enumerate((0, HALF)):
                cols = slice(v0, v0 + HALF)
                matmul_mx(
                    halves[h][:, :HALF], first_weights[g], slice(0, P),
                    x_codes[g][:, cols], x_scale_rows[:, g, cols], g == 0, g == PASSES - 1,
                )
        nc.scalar.copy(out=e_tiles[0][:, :HALF], in_=halves[0][:, :HALF])
        nc.vector.tensor_copy(out=e_tiles[0][:, HALF:T], in_=halves[1][:, :HALF])

        y_tiles = [staged[q + 3][:, :T] for q in range(TILES)]
        accs = {}

        def product(b):
            grouped = tile([P, PASSES * T], BF16, "grouped_%d" % b)
            if b <= LAST_BLOCK_CAST_BY_PASS:
                for g in range(PASSES):
                    cols = slice(g * T, (g + 1) * T)
                    cast(nc.scalar.copy, grouped[:, cols], staged[b][:, cols])
            else:
                cast(nc.scalar.copy, grouped[:], staged[b][:])
            weights = quantize(str(b), grouped[:])
            accs[b] = products.tile([P, T], F32, name="acc")
            for g in range(PASSES):
                matmul_mx(
                    accs[b][:], weights, slice(g * P, (g + 1) * P),
                    x_codes[g][:], x_scale_rows[:, g, :], g == 0, g == PASSES - 1,
                )

        def empty(b):
            q, is_w1 = divmod(b, 2)
            nc.scalar.copy(out=y_tiles[q] if is_w1 else e_tiles[q][:, :T], in_=accs[b][:])

        for b in range(1, 2 * TILES):
            product(b)
            if b >= 3:
                empty(b - 2)

        acts = tile([P, TILES, LISTS, 2, 2, P], BF16, "acts")
        last = tile([P, 2, 2, 2, P], BF16, "last")

        staging_for = dict(zip((1, 2, 3, 5, 6, 7, 8), range(1, 2 * TILES)))
        first_reusing = 14
        gathered = []

        def edge(q, d, v0, width, target):
            n = len(gathered)
            if n in staging_for:
                rows = staged[staging_for[n]][:, T:]
            elif n >= first_reusing:
                rows = gathered[n - BANKS]
            else:
                rows = tile([P, T], F32, "gathered_%d" % n)[:]
            gathered.append(rows)
            picked = rows[:, :width]
            window = e_tiles[q][:].indirect(lists[d][:, v0 // 16 : (v0 + width) // 16])
            y_part = y_tiles[q][:, v0 : v0 + width]
            if n < PLAIN_GATHERS:
                nc.vector.tensor_copy(out=picked, in_=window)
                terms = [y_part, picked]
            else:
                nc.vector.tensor_tensor(picked, window, y_part, ADD)
                terms = [picked]
            bank = sums.tile([P, T], F32, name="bank")
            blocks = width // P
            for j, term in enumerate(terms):
                for block in range(blocks):
                    cols = slice(block * P, (block + 1) * P)
                    nc.tensor.matmul(
                        bank[:, cols], term[:, cols], identity[:], is_transpose=True,
                        start=(j == 0 and block == 0),
                        stop=(j == len(terms) - 1 and block == blocks - 1),
                    )
            nc.scalar.activation(
                target.rearrange("p u h (m j) -> p u h m j", j=2),
                bank[:, :width].rearrange("p (h m u j) -> p u h m j", m=P // 2, u=2, j=2),
                SILU,
            )

        z_rows = [tile([P, 2, TILES, P // 2], BF16, "z_rows_%d" % block) for block in range(T // P)]

        def largest_into_z(block, q0, left, right):
            part = slice(block % 2 * (P // 2), (block % 2 + 1) * (P // 2))
            nc.vector.tensor_tensor(
                z_rows[block][:, :, q0 : q0 + 2, :].rearrange("p u q y -> p q u y"),
                left[:, :, :, part],
                right[:, :, :, part],
                MAX,
            )

        for d in range(LISTS):
            edge(0, d, 0, T, acts[:, 0, d])
            if d % 2 == 1:
                empty(2 * TILES - 2 + d // 2)
        for d in range(LISTS):
            edge(1, d, 0, T, acts[:, 1, d])
        pairs = tile([P, 2, 2, 2, 2, P], BF16, "pairs")
        nc.vector.tensor_tensor(pairs[:], acts[:, 0:2, 0:2], acts[:, 0:2, 2:4], MAX)
        for block in range(T // P):
            largest_into_z(block, 0, pairs[:, :, 0, :, block // 2], pairs[:, :, 1, :, block // 2])
        for q in (2, 3):
            for d in range(LISTS - 1):
                edge(q, d, 0, T, acts[:, q, d])
            if q == 2:
                edge(q, LISTS - 1, 0, T, last[:, :, 0].rearrange("p h u x -> p u h x"))
        for h in range(2):
            edge(3, LISTS - 1, h * HALF, HALF, last[:, h : h + 1, 1].rearrange("p h u x -> p u h x"))
        grouped_w3 = tile([P, N * PACK], BF16, "grouped_w3")
        cast(nc.scalar.copy, grouped_w3[:], staged_w3[:].rearrange("p t c -> p (t c)"))

        running = [acts[:, 2:4, 0, :, h] for h in range(2)]
        for d in range(1, LISTS - 1):
            for h in range(2):
                larger = tile([P, 2, 2, P], BF16, "larger_%d_%d" % (d, h))
                nc.vector.tensor_tensor(larger[:], running[h], acts[:, 2:4, d, :, h], MAX)
                running[h] = larger[:]

        grouped_z = []
        for block in range(T // P):
            largest_into_z(block, 2, running[block // 2], last[:, block // 2])
            turned = products.tile([P, T], F32, name="acc")
            for u in range(2):
                words = z_rows[block][:, u].rearrange("p q y -> p (q y)").bitcast(F32)
                nc.tensor.transpose(turned[:, u * P : (u + 1) * P], words, identity[:])
            grouped = tile([P, P * PACK], BF16, "grouped_z_%d" % block)
            nc.scalar.copy(
                out=grouped[:].bitcast(F32).rearrange("p (v u) -> p v u", u=2),
                in_=turned[:, : 2 * P].rearrange("p (u v) -> p v u", u=2),
            )
            grouped_z.append(grouped)
        weights_w3 = quantize("w3", grouped_w3[:])
        for block in range(T // P):
            codes, scales = quantize("z_%d" % block, grouped_z[block][:])
            acc = products.tile([P, T], F32, name="acc")
            matmul_mx(acc[:, :P], weights_w3, slice(0, N), codes[:], scales[:], True, True)
            result = tile([P, P], F32, "result_%d" % block)
            nc.scalar.copy(out=result[:], in_=acc[:, :P])
            nc.sync.dma_start(out=out[:, block * P : (block + 1) * P], in_=result[:])
